import numpy as np
import ml_dtypes


def mxq(x, axis, fmt="e4m3"):
    dtype, down = {"e4m3": (ml_dtypes.float8_e4m3fn, 7), "e5m2": (ml_dtypes.float8_e5m2, 14)}[fmt]
    v = np.moveaxis(np.asarray(x, np.float32).astype(ml_dtypes.bfloat16).astype(np.float64), axis, -1)
    blocks = v.reshape(v.shape[:-1] + (-1, 32))
    amax = np.abs(blocks).max(-1, keepdims=True)
    byte = np.maximum(np.where(amax > 0, np.frexp(amax)[1] - 1 + 127, 0) - down, 1)
    scale = np.exp2(byte - 127.0)
    codes = (blocks / scale).astype(np.float32).astype(dtype).astype(np.float64)
    return np.moveaxis((codes * scale).reshape(v.shape), -1, axis)


WIDE = False


def mx_kscale(k):
    if not WIDE:
        return np.ones(k)
    levels = np.array([10, -10, 5, -5, 0])
    if k % 512:
        return np.exp2(np.random.permutation(np.resize(levels, k // 32))).repeat(32)
    a = np.empty((k // 512, 16))
    for p in range(k // 512):
        a[p, :8] = np.random.permutation(np.resize(levels, 8))
        for g in range(8):
            far = levels[np.abs(levels - a[p, g]) >= 10]
            a[p, g + 8] = far[np.random.randint(len(far))]
    return np.exp2(a.ravel()).repeat(32)


def f64(x):
    return np.asarray(x).astype(np.float64)


def striped(idx):
    return np.tile(np.asarray(idx).reshape(-1, 16).T, (8, 1)).astype(np.uint16)


def unstriped(offs):
    return offs[:16].T.reshape(-1).astype(np.int64)


E2M1 = np.array([0.0, 0.5, 1.0, 1.5, 2.0, 3.0, 4.0, 6.0, -0.0, -0.5, -1.0, -1.5, -2.0, -3.0, -4.0, -6.0])


def pack_weight(w, fmt):
    k, n = w.shape
    w = f64(np.asarray(w, np.float32).astype(ml_dtypes.bfloat16)).reshape(k // 32, 32, n)
    amax = np.abs(w).max(1)
    if fmt == "e4m3":
        byte = np.frexp(amax)[1] - 1 + 127 - 7
    else:
        mant, ex = np.frexp(amax / 6.0)
        byte = np.where(mant > 0.5, ex, ex - 1) + 127
    byte = np.clip(np.where(amax > 0, byte, 1), 1, 254)
    scaled = (w * np.exp2(127.0 - byte)[:, None, :]).reshape(k, n).astype(np.float32)
    by_word = np.ascontiguousarray(scaled.reshape(k // 512, 128, 4, n).transpose(0, 1, 3, 2))
    if fmt == "e4m3":
        words = by_word.astype(ml_dtypes.float8_e4m3fn).view(np.uint8)
    else:
        c = by_word.astype(ml_dtypes.float4_e2m1fn).view(np.uint8) & 0xF
        words = (c[..., 0::2] | (c[..., 1::2] << 4)).reshape(k // 512, 128, 2 * n)
    return np.ascontiguousarray(words), np.ascontiguousarray(byte.astype(np.uint8).reshape(k // 512, 16, n))


def unpack_weight(words, scales, fmt):
    g, _, n = scales.shape
    words = np.ascontiguousarray(words).reshape(g, 128, n, -1)
    if fmt == "e4m3":
        vals = words.view(ml_dtypes.float8_e4m3fn).astype(np.float64)
    else:
        nib = np.empty((g, 128, n, 4), np.uint8)
        nib[..., 0::2] = words & 0xF
        nib[..., 1::2] = words >> 4
        vals = E2M1[nib]
    vals = vals * np.repeat(np.exp2(scales.astype(np.float64) - 127.0), 8, axis=1)[..., None]
    return vals.transpose(0, 1, 3, 2).reshape(g * 512, n)


def bf(x):
    return np.asarray(x, np.float32).astype(ml_dtypes.bfloat16)


def planes(Y):
    r, m = Y.shape
    b = f64(bf(Y)).reshape(r // 32, 32, m)
    amax = np.abs(b).max(1)
    byte = np.clip(np.where(amax > 0, np.frexp(amax)[1] - 1 + 127 - 7, 1), 1, 254)
    codes = (b * np.exp2(127.0 - byte)[:, None, :]).reshape(r, m).astype(np.float32).astype(ml_dtypes.float8_e4m3fn).view(np.uint8)
    words = codes.reshape(r // 512, 128, 4, m).transpose(0, 1, 3, 2)
    return np.ascontiguousarray(words), np.ascontiguousarray(byte.astype(np.uint8).reshape(r // 512, 16, m))


D, T, I, Q, E, V = 512, 2048, 512, 256, 512, 32


def setup_inputs():
    n = np.random.standard_normal
    idx = np.random.permutation(T)[:I]
    fd = mx_kscale(D)
    fi = mx_kscale(I)
    ti = np.ones(T)
    ti[idx] = fi
    keysp = pack_weight(n((D, T)) / fd[:, None], "e2m1")
    return {
        "query": (n((D, Q)) * 0.8 / np.sqrt(D) * fd[:, None]).astype(np.float32),
        "keys_words": keysp[0],
        "keys_scales": keysp[1],
        "lam": (np.random.uniform(0.05, 0.12, (1, Q))).astype(np.float32),
        "width": (np.random.uniform(0.3, 0.8, (Q, 1))).astype(np.float32),
        "os": (np.random.uniform(4.0, 16.0, (1, I)) * fi).astype(np.float32),
        "vals": (n((E, T)) / ti).astype(np.float32),
        "floors": (n((E, Q)) * 1.5).astype(np.float32),
        "offs": striped(idx),
    }


def reference(query, keys_words, keys_scales, lam, width, os, vals, floors, offs):
    idx = unstriped(offs)
    keysu = unpack_weight(keys_words, keys_scales, "e2m1")
    keysidxg = keysu[:, idx]
    queryq = mxq(f64(query), 0, "e4m3")
    a0 = keysidxg.T @ queryq
    ag = a0.reshape(I, V, Q // V).sum(axis=2)
    ar = np.repeat(ag, Q // V, axis=1)
    s0 = a0 - ar * f64(lam)
    s = s0.T
    ce = (s - np.mean(s, axis=1, keepdims=True)) / f64(width)
    p = 1.0 / (np.square(ce) + 1.0)
    w = p / np.sum(p, axis=1, keepdims=True)
    wo1 = w * f64(os)
    wt1 = wo1.T
    vt1 = f64(vals)[:, idx].T
    vt1q = mxq(vt1, 0, "e4m3")
    wt1q = mxq(wt1, 0, "e4m3")
    o = vt1q.T @ wt1q
    y = np.maximum(o, f64(floors)) + np.minimum(o, f64(floors)) * 0.1
    words, scales = planes(y)
    return y, words, scales

@@ -1,0 +1,280 @@
+from contextlib import ExitStack
+
+import concourse.mybir as mybir
+from concourse.masks import make_identity
+
+D, T, I, Q, E, GROUP = 512, 2048, 512, 256, 512, 8
+FLOPS = 2 * D * I * Q + 2 * I * E * Q
+
+F32 = mybir.dt.float32
+BF16 = mybir.dt.bfloat16
+I32 = mybir.dt.int32
+U32 = mybir.dt.uint32
+U16 = mybir.dt.uint16
+U8 = mybir.dt.uint8
+FP8X4 = mybir.dt.float8_e4m3fn_x4
+FP4X4 = mybir.dt.float4_e2m1fn_x4
+ALU = mybir.AluOpType
+ACT = mybir.ActivationFunctionType
+AX = mybir.AxisListType
+
+P = 128
+PACK = 4
+HALVES = Q // P
+
+
+def tile_attend_beyondgroup_typical_atleast_pl_kernel(
+    tc, query, keys_words, keys_scales, lam, width, slot_factor, vals, floors, offs, out_0, out_1, out_2
+):
+    nc = tc.nc
+    with ExitStack() as ctx:
+        held = ctx.enter_context(tc.tile_pool(name="held", bufs=1))
+        slots = ctx.enter_context(tc.tile_pool(name="slots", bufs=1))
+        psum = ctx.enter_context(tc.psum_pool(name="psum", bufs=1))
+
+        def sb(name, shape, dtype):
+            return held.tile(shape, dtype, name=name, align_bytes=64)
+
+        def bank(name, tag, shape):
+            return psum.tile(shape, F32, name=name, tag=tag)
+
+        offsets = held.tile([P, I // 16], U16, name="offsets")
+        nc.sync.dma_start(offsets[:], offs)
+
+        key_scales = slots.tile([P, T], U8, name="key_scales", tag="b")
+        nc.vector.memset(key_scales[:].bitcast(I32), 0)
+        key_words = slots.tile([P, T], U16, name="key_words", tag="a")
+        nc.sync.dma_start(key_words[:].bitcast(I32), keys_words[0].bitcast(I32))
+        for quad in range(4):
+            nc.scalar.dma_start(
+                key_scales[32 * quad : 32 * quad + 4, :].bitcast(I32),
+                keys_scales[0, 4 * quad : 4 * quad + 4, :].bitcast(I32),
+            )
+        q_raw = slots.tile([P, PACK, Q], F32, name="q_raw", tag="c")
+        nc.sync.dma_start(q_raw[:], query.rearrange("(p t) q -> p t q", t=PACK))
+
+        vals_rows = vals.rearrange("(p j) t -> j p t", j=PACK)
+        windows = []
+
+        def load_vals(j, tag):
+            window = slots.tile([P, T], F32, name="vals%d" % j, tag=tag)
+            nc.sync.dma_start(window[:], vals_rows[j])
+            windows.append(window)
+
+        load_vals(0, "d")
+
+        one = sb("one", [P, 1], F32)
+        nc.vector.memset(one[:], 1.0)
+        warm = sb("warm", [P, 1], F32)
+        nc.scalar.activation(warm[:], one[:], ACT.Abs_reciprocal_sqrt, bias=one[:])
+
+        ident = sb("ident", [P, P], F32)
+        make_identity(nc, ident[:])
+        vec_rows = sb("vec_rows", [P, P], F32)
+        nc.vector.memset(vec_rows[:], 0.0)
+        nc.scalar.dma_start(vec_rows[0:2, :], lam.rearrange("o (h m) -> (o h) m", m=P))
+        nc.scalar.dma_start(vec_rows[2:4, :], width.rearrange("(h m) o -> h (m o)", m=P))
+        nc.scalar.dma_start(vec_rows[4:8, :], slot_factor.rearrange("o (c m) -> (o c) m", m=P))
+
+        k_words = sb("k_words", [P, I], U16)
+        k_scales = sb("k_scales", [P, I], U8)
+        nc.vector.tensor_copy(k_words[:], key_words[:].indirect(offsets[:]))
+        nc.vector.tensor_copy(k_scales[:], key_scales[:].indirect(offsets[:]))
+        load_vals(1, "a")
+        load_vals(2, "b")
+
+        q_codes = sb("q_codes", [P, Q], U32)
+        q_scales = sb("q_scales", [P, Q], U8)
+        q_grouped = []
+        for h in range(HALVES):
+            g = sb("q_grouped%d" % h, [P, P, PACK], BF16)
+            nc.scalar.copy(g[:], q_raw[:, :, h * P : (h + 1) * P].rearrange("p t q -> p q t"))
+            q_grouped.append(g)
+        for h in range(HALVES):
+            cols = slice(h * P, (h + 1) * P)
+            nc.vector.quantize_mx(
+                out=q_codes[:, cols].bitcast(FP8X4),
+                scales=q_scales[:, cols],
+                in_=q_grouped[h][:].rearrange("p q t -> p (q t)"),
+            )
+        load_vals(3, "c")
+
+        vec_turned = bank("vec_turned", "v0", [P, P])
+        nc.tensor.transpose(vec_turned[:], vec_rows[:], ident[:])
+        vec_cols = sb("vec_cols", [P, 8], F32)
+        nc.scalar.copy(vec_cols[:], vec_turned[:, 0:8])
+        lam_row = bank("lam_row", "lam", [P, HALVES, P])
+        for h in range(HALVES):
+            nc.tensor.transpose(lam_row[:, h, :], vec_cols[:, h : h + 1].to_broadcast([P, P]), ident[:])
+        os_row = bank("os_row", "os", [P, PACK, P])
+        for c in range(PACK):
+            nc.tensor.transpose(os_row[:, c, :], vec_cols[:, 4 + c : 5 + c].to_broadcast([P, P]), ident[:])
+        inv_width = sb("inv_width", [P, HALVES], F32)
+        nc.vector.reciprocal(inv_width[:], vec_cols[:, 2:4])
+        mean_scale = sb("mean_scale", [P, HALVES], F32)
+        nc.vector.tensor_scalar(mean_scale[:], inv_width[:], -1.0 / I, None, ALU.mult)
+
+        scores = []
+        for h in range(HALVES):
+            cols = slice(h * P, (h + 1) * P)
+            acc = bank("scores%d" % h, "s%d" % h, [P, PACK, P])
+            for c in range(PACK):
+                nc.tensor.matmul_mx(
+                    out=acc[:, c, :],
+                    lhsT=k_words[:, c * P : (c + 1) * P].bitcast(FP4X4),
+                    lhsT_scale=k_scales[:, c * P : (c + 1) * P],
+                    rhs=q_codes[:, cols].bitcast(FP8X4),
+                    rhs_scale=q_scales[:, cols],
+                    start=True,
+                    stop=True,
+                )
+            scores.append(acc)
+
+        turned = []
+        for h in range(HALVES):
+            group_sum = sb("group_sum%d" % h, [P, PACK, P // GROUP], F32)
+            nc.vector.tensor_reduce(
+                group_sum[:], scores[h][:].rearrange("p c (v j) -> p c v j", j=GROUP), AX.X, ALU.add
+            )
+            minus_a0 = sb("minus_a0%d" % h, [P, PACK, P], F32)
+            nc.scalar.activation(minus_a0[:], scores[h][:], ACT.Copy, scale=-1.0)
+            share = sb("share%d" % h, [P, PACK, P], F32)
+            nc.vector.tensor_tensor(
+                share[:].rearrange("p c (v j) -> p c v j", j=GROUP),
+                group_sum[:].unsqueeze(3).to_broadcast([P, PACK, P // GROUP, GROUP]),
+                lam_row[:, h, :]
+                .rearrange("p (v j) -> p v j", j=GROUP)
+                .unsqueeze(1)
+                .to_broadcast([P, PACK, P // GROUP, GROUP]),
+                ALU.mult,
+            )
+            acc = bank("turned%d" % h, "t%d" % h, [P, PACK, P])
+            for c in range(PACK):
+                nc.tensor.matmul(
+                    acc[:, c, :], minus_a0[:, c, :], ident[:], start=(c == 0), stop=False, is_transpose=True
+                )
+            for c in range(PACK):
+                nc.tensor.matmul(
+                    acc[:, c, :], share[:, c, :], ident[:], start=False, stop=(c == PACK - 1), is_transpose=True
+                )
+            turned.append(acc)
+
+        v_codes = sb("v_codes", [P, E], U32)
+        v_scales = sb("v_scales", [P, E], U8)
+
+        def turn_words(src, acc, dst):
+            words = src[:].bitcast(F32)
+            for u in range(2):
+                nc.tensor.transpose(acc[:, u, :], words[:, u : I // 2 : 2], ident[:])
+            nc.scalar.copy(
+                dst[:].bitcast(F32).rearrange("p (m u) -> p m u", u=2), acc[:].rearrange("p u m -> p m u")
+            )
+
+        def gather_vals(j):
+            picked = sb("picked%d" % j, [P, I], BF16)
+            nc.vector.tensor_copy(picked[:], windows[j][:].indirect(offsets[:]))
+            grouped = sb("v_grouped%d" % j, [P, P * PACK], BF16)
+            turn_words(picked, bank("v_turned%d" % j, "v%d" % (j % 2), [P, 2, P]), grouped)
+            return grouped
+
+        def quantize_vals(j, grouped):
+            cols = slice(j * P, (j + 1) * P)
+            nc.vector.quantize_mx(out=v_codes[:, cols].bitcast(FP8X4), scales=v_scales[:, cols], in_=grouped[:])
+
+        def parts(h):
+            scaled = sb("scaled%d" % h, [P, I], F32)
+            centre = sb("centre%d" % h, [P, 1], F32)
+            nc.scalar.activation(
+                scaled[:],
+                turned[h][:].rearrange("p c m -> p (c m)"),
+                ACT.Identity,
+                scale=mean_scale[:, h : h + 1],
+                accum_out=centre[:],
+            )
+            z2 = sb("z2_%d" % h, [P, I], F32)
+            nc.scalar.activation(z2[:], scaled[:], ACT.Square, bias=centre[:], scale=-float(I))
+            root = sb("root%d" % h, [P, I], F32)
+            nc.scalar.activation(root[:], z2[:], ACT.Abs_reciprocal_sqrt, bias=one[:])
+            part = sb("part%d" % h, [P, I], F32)
+            total = sb("total%d" % h, [P, 1], F32)
+            nc.scalar.activation(part[:], root[:], ACT.Square, accum_out=total[:])
+            return part, total
+
+        w_codes = sb("w_codes", [P, Q], U32)
+        w_scales = sb("w_scales", [P, Q], U8)
+
+        def weights(h, part, total):
+            inv_total = sb("inv_total%d" % h, [P, 1], F32)
+            nc.vector.reciprocal(inv_total[:], total[:])
+            w = sb("w%d" % h, [P, I], BF16)
+            nc.vector.scalar_tensor_tensor(
+                w[:],
+                part[:],
+                inv_total[:],
+                os_row[:].rearrange("p c m -> p (c m)"),
+                ALU.mult,
+                ALU.mult,
+            )
+            grouped = sb("w_grouped%d" % h, [P, P * PACK], BF16)
+            turn_words(w, bank("w_turned%d" % h, "lam", [P, 2, P]), grouped)
+            return grouped
+
+        def quantize_weights(h, grouped):
+            cols = slice(h * P, (h + 1) * P)
+            nc.vector.quantize_mx(out=w_codes[:, cols].bitcast(FP8X4), scales=w_scales[:, cols], in_=grouped[:])
+
+        part0 = parts(0)
+        g0 = gather_vals(0)
+        floor = slots.tile([P, PACK, Q], F32, name="floor", tag="d")
+        nc.sync.dma_start(floor[:], floors.rearrange("(p j) q -> p j q", j=PACK))
+        part1 = parts(1)
+        g1 = gather_vals(1)
+        quantize_vals(0, g0)
+        w0 = weights(0, *part0)
+        quantize_vals(1, g1)
+        g2 = gather_vals(2)
+        quantize_weights(0, w0)
+        w1 = weights(1, *part1)
+        quantize_vals(2, g2)
+        g3 = gather_vals(3)
+        quantize_weights(1, w1)
+        quantize_vals(3, g3)
+
+        y = sb("y", [P, PACK, Q], F32)
+        y_codes = sb("y_codes", [P, Q], U32)
+        y_scales = sb("y_scales", [P, Q], U8)
+        y_rows = out_0.rearrange("(p j) q -> p j q", j=PACK)
+        code_rows = out_1[0].rearrange("p c t -> p (c t)").bitcast(I32)
+        for h in range(HALVES):
+            cols = slice(h * P, (h + 1) * P)
+            acc = bank("o%d" % h, "s%d" % h, [P, PACK, P])
+            for j in range(PACK):
+                nc.tensor.matmul_mx(
+                    out=acc[:, j, :],
+                    lhsT=v_codes[:, j * P : (j + 1) * P].bitcast(FP8X4),
+                    lhsT_scale=v_scales[:, j * P : (j + 1) * P],
+                    rhs=w_codes[:, cols].bitcast(FP8X4),
+                    rhs_scale=w_scales[:, cols],
+                    start=True,
+                    stop=True,
+                )
+            larger = sb("larger%d" % h, [P, PACK, P], F32)
+            smaller = sb("smaller%d" % h, [P, PACK, P], F32)
+            nc.vector.tensor_tensor(larger[:], acc[:], floor[:, :, cols], ALU.max)
+            nc.vector.tensor_tensor(smaller[:], acc[:], floor[:, :, cols], ALU.min)
+            nc.vector.scalar_tensor_tensor(y[:, :, cols], smaller[:], 0.1, larger[:], ALU.mult, ALU.add)
+            nc.sync.dma_start(y_rows[:, :, cols], y[:, :, cols])
+            grouped = sb("y_grouped%d" % h, [P, P, PACK], BF16)
+            nc.scalar.copy(grouped[:], y[:, :, cols].rearrange("p j q -> p q j"))
+            nc.vector.quantize_mx(
+                out=y_codes[:, cols].bitcast(FP8X4),
+                scales=y_scales[:, cols],
+                in_=grouped[:].rearrange("p q j -> p (q j)"),
+            )
+            nc.sync.dma_start(code_rows[:, cols], y_codes[:, cols].bitcast(I32))
+        for quad in range(4):
+            queue = nc.sync if quad % 2 else nc.scalar
+            queue.dma_start(
+                out_2[0, 4 * quad : 4 * quad + 4, :].bitcast(I32),
+                y_scales[32 * quad : 32 * quad + 4, :].bitcast(I32),
+            )

@@ -32,8 +32,8 @@ def tile_attend_beyondgroup_typical_atleast_pl_kernel(
         slots = ctx.enter_context(tc.tile_pool(name="slots", bufs=1))
         psum = ctx.enter_context(tc.psum_pool(name="psum", bufs=1))
 
-        def sb(name, shape, dtype):
-            return held.tile(shape, dtype, name=name, align_bytes=64)
+        def sb(name, shape, dtype, tag=None):
+            return held.tile(shape, dtype, name=name, tag=tag or name, align_bytes=64)
 
         def bank(name, tag, shape):
             return psum.tile(shape, F32, name=name, tag=tag)
@@ -46,7 +46,7 @@ def tile_attend_beyondgroup_typical_atleast_pl_kernel(
         key_words = slots.tile([P, T], U16, name="key_words", tag="a")
         nc.sync.dma_start(key_words[:].bitcast(I32), keys_words[0].bitcast(I32))
         for quad in range(4):
-            nc.scalar.dma_start(
+            nc.sync.dma_start(
                 key_scales[32 * quad : 32 * quad + 4, :].bitcast(I32),
                 keys_scales[0, 4 * quad : 4 * quad + 4, :].bitcast(I32),
             )
@@ -61,27 +61,37 @@ def tile_attend_beyondgroup_typical_atleast_pl_kernel(
             nc.sync.dma_start(window[:], vals_rows[j])
             windows.append(window)
 
-        load_vals(0, "d")
-
         one = sb("one", [P, 1], F32)
         nc.vector.memset(one[:], 1.0)
-        warm = sb("warm", [P, 1], F32)
-        nc.scalar.activation(warm[:], one[:], ACT.Abs_reciprocal_sqrt, bias=one[:])
+        seed = slots.tile([P, 1], F32, name="seed", tag="e")
+        nc.vector.memset(seed[:], 1.0)
+        warm = slots.tile([P, 1], F32, name="warm", tag="d")
+        nc.scalar.activation(warm[:], seed[:], ACT.Abs_reciprocal_sqrt, bias=one[:])
+        load_vals(0, "d")
+        load_vals(1, "e")
 
+        lam_rows = sb("lam_rows", [P, P], F32)
+        rest_rows = sb("rest_rows", [P, P], F32)
+        nc.gpsimd.memset(lam_rows[:], 0.0)
+        nc.gpsimd.memset(rest_rows[:], 0.0)
         ident = sb("ident", [P, P], F32)
         make_identity(nc, ident[:])
-        vec_rows = sb("vec_rows", [P, P], F32)
-        nc.vector.memset(vec_rows[:], 0.0)
-        nc.scalar.dma_start(vec_rows[0:2, :], lam.rearrange("o (h m) -> (o h) m", m=P))
-        nc.scalar.dma_start(vec_rows[2:4, :], width.rearrange("(h m) o -> h (m o)", m=P))
-        nc.scalar.dma_start(vec_rows[4:8, :], slot_factor.rearrange("o (c m) -> (o c) m", m=P))
+        nc.scalar.dma_start(lam_rows[0:2, :], lam.rearrange("o (h m) -> (o h) m", m=P))
+        nc.gpsimd.dma_start(rest_rows[0:2, :], width.rearrange("(h m) o -> h (m o)", m=P))
+        nc.gpsimd.dma_start(rest_rows[2:6, :], slot_factor.rearrange("o (c m) -> (o c) m", m=P))
+        lam_turned = bank("lam_turned", "t0", [P, P])
+        nc.tensor.transpose(lam_turned[:], lam_rows[:], ident[:])
+        lam_col = sb("lam_col", [P, HALVES], F32)
+        nc.scalar.copy(lam_col[:], lam_turned[:, 0:HALVES])
+        lam_row = bank("lam_row", "lam", [P, HALVES, P])
+        for h in range(HALVES):
+            nc.tensor.transpose(lam_row[:, h, :], lam_col[:, h : h + 1].to_broadcast([P, P]), ident[:])
 
         k_words = sb("k_words", [P, I], U16)
         k_scales = sb("k_scales", [P, I], U8)
         nc.vector.tensor_copy(k_words[:], key_words[:].indirect(offsets[:]))
         nc.vector.tensor_copy(k_scales[:], key_scales[:].indirect(offsets[:]))
-        load_vals(1, "a")
-        load_vals(2, "b")
+        load_vals(2, "a")
 
         q_codes = sb("q_codes", [P, Q], U32)
         q_scales = sb("q_scales", [P, Q], U8)
@@ -97,22 +107,15 @@ def tile_attend_beyondgroup_typical_atleast_pl_kernel(
                 scales=q_scales[:, cols],
                 in_=q_grouped[h][:].rearrange("p q t -> p (q t)"),
             )
-        load_vals(3, "c")
 
-        vec_turned = bank("vec_turned", "v0", [P, P])
-        nc.tensor.transpose(vec_turned[:], vec_rows[:], ident[:])
-        vec_cols = sb("vec_cols", [P, 8], F32)
-        nc.scalar.copy(vec_cols[:], vec_turned[:, 0:8])
-        lam_row = bank("lam_row", "lam", [P, HALVES, P])
-        for h in range(HALVES):
-            nc.tensor.transpose(lam_row[:, h, :], vec_cols[:, h : h + 1].to_broadcast([P, P]), ident[:])
-        os_row = bank("os_row", "os", [P, PACK, P])
-        for c in range(PACK):
-            nc.tensor.transpose(os_row[:, c, :], vec_cols[:, 4 + c : 5 + c].to_broadcast([P, P]), ident[:])
-        inv_width = sb("inv_width", [P, HALVES], F32)
-        nc.vector.reciprocal(inv_width[:], vec_cols[:, 2:4])
-        mean_scale = sb("mean_scale", [P, HALVES], F32)
-        nc.vector.tensor_scalar(mean_scale[:], inv_width[:], -1.0 / I, None, ALU.mult)
+        floor_rows = floors.rearrange("(p j) q -> p j q", j=PACK)
+        floor = slots.tile([P, PACK, Q], F32, name="floor", tag="c")
+        nc.sync.dma_start(floor[:], floor_rows)
+        load_vals(3, "b")
+        rest_turned = bank("rest_turned", "v1", [P, P])
+        nc.tensor.transpose(rest_turned[:], rest_rows[:], ident[:])
+        rest_col = sb("rest_col", [P, HALVES + PACK], F32, "q_grouped0")
+        nc.scalar.copy(rest_col[:], rest_turned[:, 0 : HALVES + PACK])
 
         scores = []
         for h in range(HALVES):
@@ -159,6 +162,14 @@ def tile_attend_beyondgroup_typical_atleast_pl_kernel(
                 )
             turned.append(acc)
 
+        inv_width = sb("inv_width", [P, HALVES], F32, "group_sum0")
+        nc.vector.reciprocal(inv_width[:], rest_col[:, 0:HALVES])
+        mean_scale = sb("mean_scale", [P, HALVES], F32)
+        nc.vector.tensor_scalar(mean_scale[:], inv_width[:], -1.0 / I, None, ALU.mult)
+        os_row = bank("os_row", "os", [P, PACK, P])
+        for t in range(PACK):
+            nc.tensor.transpose(os_row[:, t, :], rest_col[:, HALVES + t : HALVES + t + 1].to_broadcast([P, P]), ident[:])
+
         v_codes = sb("v_codes", [P, E], U32)
         v_scales = sb("v_scales", [P, E], U8)
 
@@ -171,7 +182,10 @@ def tile_attend_beyondgroup_typical_atleast_pl_kernel(
             )
 
         def gather_vals(j):
-            picked = sb("picked%d" % j, [P, I], BF16)
+            if j == 2:
+                picked = slots.tile([P, I], BF16, name="picked2", tag="e")
+            else:
+                picked = sb("picked%d" % j, [P, I], BF16, ["q_grouped1", "group_sum1", "", "inv_total0"][j])
             nc.vector.tensor_copy(picked[:], windows[j][:].indirect(offsets[:]))
             grouped = sb("v_grouped%d" % j, [P, P * PACK], BF16)
             turn_words(picked, bank("v_turned%d" % j, "v%d" % (j % 2), [P, 2, P]), grouped)
@@ -223,34 +237,16 @@ def tile_attend_beyondgroup_typical_atleast_pl_kernel(
             cols = slice(h * P, (h + 1) * P)
             nc.vector.quantize_mx(out=w_codes[:, cols].bitcast(FP8X4), scales=w_scales[:, cols], in_=grouped[:])
 
-        part0 = parts(0)
-        g0 = gather_vals(0)
-        floor = slots.tile([P, PACK, Q], F32, name="floor", tag="d")
-        nc.sync.dma_start(floor[:], floors.rearrange("(p j) q -> p j q", j=PACK))
-        part1 = parts(1)
-        g1 = gather_vals(1)
-        quantize_vals(0, g0)
-        w0 = weights(0, *part0)
-        quantize_vals(1, g1)
-        g2 = gather_vals(2)
-        quantize_weights(0, w0)
-        w1 = weights(1, *part1)
-        quantize_vals(2, g2)
-        g3 = gather_vals(3)
-        quantize_weights(1, w1)
-        quantize_vals(3, g3)
-
         y = sb("y", [P, PACK, Q], F32)
-        y_codes = sb("y_codes", [P, Q], U32)
-        y_scales = sb("y_scales", [P, Q], U8)
         y_rows = out_0.rearrange("(p j) q -> p j q", j=PACK)
-        code_rows = out_1[0].rearrange("p c t -> p (c t)").bitcast(I32)
-        for h in range(HALVES):
-            cols = slice(h * P, (h + 1) * P)
-            acc = bank("o%d" % h, "s%d" % h, [P, PACK, P])
-            for j in range(PACK):
+
+        def finish(name, tag, js, cols, floor):
+            n = cols.stop - cols.start
+            shape = [P, len(js), n]
+            acc = bank("o_" + name, tag, shape)
+            for k, j in enumerate(js):
                 nc.tensor.matmul_mx(
-                    out=acc[:, j, :],
+                    out=acc[:, k, :],
                     lhsT=v_codes[:, j * P : (j + 1) * P].bitcast(FP8X4),
                     lhsT_scale=v_scales[:, j * P : (j + 1) * P],
                     rhs=w_codes[:, cols].bitcast(FP8X4),
@@ -258,20 +254,48 @@ def tile_attend_beyondgroup_typical_atleast_pl_kernel(
                     start=True,
                     stop=True,
                 )
-            larger = sb("larger%d" % h, [P, PACK, P], F32)
-            smaller = sb("smaller%d" % h, [P, PACK, P], F32)
-            nc.vector.tensor_tensor(larger[:], acc[:], floor[:, :, cols], ALU.max)
-            nc.vector.tensor_tensor(smaller[:], acc[:], floor[:, :, cols], ALU.min)
-            nc.vector.scalar_tensor_tensor(y[:, :, cols], smaller[:], 0.1, larger[:], ALU.mult, ALU.add)
-            nc.sync.dma_start(y_rows[:, :, cols], y[:, :, cols])
+            larger = sb("larger_" + name, shape, F32)
+            smaller = sb("smaller_" + name, shape, F32)
+            rows = slice(js[0], js[-1] + 1)
+            nc.vector.tensor_tensor(smaller[:], acc[:], floor, ALU.min)
+            nc.vector.tensor_tensor(larger[:], acc[:], floor, ALU.max)
+            nc.vector.scalar_tensor_tensor(y[:, rows, cols], smaller[:], 0.1, larger[:], ALU.mult, ALU.add)
+            nc.sync.dma_start(y_rows[:, rows, cols], y[:, rows, cols])
+
+        y_codes = sb("y_codes", [P, Q], U32)
+        y_scales = sb("y_scales", [P, Q], U8)
+        code_rows = out_1[0].rearrange("p c t -> p (c t)").bitcast(I32)
+
+        def planes(h, copy):
+            cols = slice(h * P, (h + 1) * P)
             grouped = sb("y_grouped%d" % h, [P, P, PACK], BF16)
-            nc.scalar.copy(grouped[:], y[:, :, cols].rearrange("p j q -> p q j"))
+            copy(grouped[:], y[:, :, cols].rearrange("p j q -> p q j"))
             nc.vector.quantize_mx(
                 out=y_codes[:, cols].bitcast(FP8X4),
                 scales=y_scales[:, cols],
                 in_=grouped[:].rearrange("p q j -> p (q j)"),
             )
             nc.sync.dma_start(code_rows[:, cols], y_codes[:, cols].bitcast(I32))
+
+        g0 = gather_vals(0)
+        part0 = parts(0)
+        part1 = parts(1)
+        g1 = gather_vals(1)
+        quantize_vals(0, g0)
+        g2 = gather_vals(2)
+        quantize_vals(1, g1)
+        w0 = weights(0, *part0)
+        quantize_vals(2, g2)
+        quantize_weights(0, w0)
+        finish("a", "s0", [0, 1, 2], slice(0, P), floor[:, 0:3, 0:P])
+        g3 = gather_vals(3)
+        w1 = weights(1, *part1)
+        quantize_vals(3, g3)
+        finish("b", "t0", [3], slice(0, P), floor[:, 3:4, 0:P])
+        quantize_weights(1, w1)
+        planes(0, nc.scalar.copy)
+        finish("c", "s1", [0, 1, 2, 3], slice(P, Q), floor[:, :, P:Q])
+        planes(1, nc.vector.tensor_copy)
         for quad in range(4):
             queue = nc.sync if quad % 2 else nc.scalar
             queue.dma_start(

@@ -41,6 +41,10 @@ def tile_attend_beyondgroup_typical_atleast_pl_kernel(
         offsets = held.tile([P, I // 16], U16, name="offsets")
         nc.sync.dma_start(offsets[:], offs)
 
+        lam_rows = sb("lam_rows", [P, P], F32)
+        nc.gpsimd.memset(lam_rows[:], 0.0)
+        nc.scalar.dma_start(lam_rows[0:2, :], lam.rearrange("o (h m) -> (o h) m", m=P))
+        nc.gpsimd.dma_start(lam_rows[2:4, :], width.rearrange("(h m) o -> h (m o)", m=P))
         key_scales = slots.tile([P, T], U8, name="key_scales", tag="b")
         nc.vector.memset(key_scales[:].bitcast(I32), 0)
         key_words = slots.tile([P, T], U16, name="key_words", tag="a")
@@ -70,19 +74,15 @@ def tile_attend_beyondgroup_typical_atleast_pl_kernel(
         load_vals(0, "d")
         load_vals(1, "e")
 
-        lam_rows = sb("lam_rows", [P, P], F32)
         rest_rows = sb("rest_rows", [P, P], F32)
-        nc.gpsimd.memset(lam_rows[:], 0.0)
-        nc.gpsimd.memset(rest_rows[:], 0.0)
         ident = sb("ident", [P, P], F32)
         make_identity(nc, ident[:])
-        nc.scalar.dma_start(lam_rows[0:2, :], lam.rearrange("o (h m) -> (o h) m", m=P))
-        nc.gpsimd.dma_start(rest_rows[0:2, :], width.rearrange("(h m) o -> h (m o)", m=P))
-        nc.gpsimd.dma_start(rest_rows[2:6, :], slot_factor.rearrange("o (c m) -> (o c) m", m=P))
+        nc.gpsimd.memset(rest_rows[:], 0.0)
+        nc.gpsimd.dma_start(rest_rows[0:4, :], slot_factor.rearrange("o (c m) -> (o c) m", m=P))
         lam_turned = bank("lam_turned", "t0", [P, P])
         nc.tensor.transpose(lam_turned[:], lam_rows[:], ident[:])
-        lam_col = sb("lam_col", [P, HALVES], F32)
-        nc.scalar.copy(lam_col[:], lam_turned[:, 0:HALVES])
+        lam_col = sb("lam_col", [P, 2 * HALVES], F32)
+        nc.scalar.copy(lam_col[:], lam_turned[:, 0 : 2 * HALVES])
         lam_row = bank("lam_row", "lam", [P, HALVES, P])
         for h in range(HALVES):
             nc.tensor.transpose(lam_row[:, h, :], lam_col[:, h : h + 1].to_broadcast([P, P]), ident[:])
@@ -108,14 +108,10 @@ def tile_attend_beyondgroup_typical_atleast_pl_kernel(
                 in_=q_grouped[h][:].rearrange("p q t -> p (q t)"),
             )
 
+        load_vals(3, "c")
         floor_rows = floors.rearrange("(p j) q -> p j q", j=PACK)
-        floor = slots.tile([P, PACK, Q], F32, name="floor", tag="c")
+        floor = slots.tile([P, PACK, Q], F32, name="floor", tag="b")
         nc.sync.dma_start(floor[:], floor_rows)
-        load_vals(3, "b")
-        rest_turned = bank("rest_turned", "v1", [P, P])
-        nc.tensor.transpose(rest_turned[:], rest_rows[:], ident[:])
-        rest_col = sb("rest_col", [P, HALVES + PACK], F32, "q_grouped0")
-        nc.scalar.copy(rest_col[:], rest_turned[:, 0 : HALVES + PACK])
 
         scores = []
         for h in range(HALVES):
@@ -162,13 +158,17 @@ def tile_attend_beyondgroup_typical_atleast_pl_kernel(
                 )
             turned.append(acc)
 
-        inv_width = sb("inv_width", [P, HALVES], F32, "group_sum0")
-        nc.vector.reciprocal(inv_width[:], rest_col[:, 0:HALVES])
+        inv_width = sb("inv_width", [P, HALVES], F32, "q_grouped0")
+        nc.vector.reciprocal(inv_width[:], lam_col[:, HALVES : 2 * HALVES])
         mean_scale = sb("mean_scale", [P, HALVES], F32)
         nc.vector.tensor_scalar(mean_scale[:], inv_width[:], -1.0 / I, None, ALU.mult)
+        rest_turned = bank("rest_turned", "v1", [P, P])
+        nc.tensor.transpose(rest_turned[:], rest_rows[:], ident[:])
+        rest_col = sb("rest_col", [P, PACK], F32, "group_sum0")
+        nc.scalar.copy(rest_col[:], rest_turned[:, 0:PACK])
         os_row = bank("os_row", "os", [P, PACK, P])
         for t in range(PACK):
-            nc.tensor.transpose(os_row[:, t, :], rest_col[:, HALVES + t : HALVES + t + 1].to_broadcast([P, P]), ident[:])
+            nc.tensor.transpose(os_row[:, t, :], rest_col[:, t : t + 1].to_broadcast([P, P]), ident[:])
 
         v_codes = sb("v_codes", [P, E], U32)
         v_scales = sb("v_scales", [P, E], U8)
@@ -185,9 +185,9 @@ def tile_attend_beyondgroup_typical_atleast_pl_kernel(
             if j == 2:
                 picked = slots.tile([P, I], BF16, name="picked2", tag="e")
             else:
-                picked = sb("picked%d" % j, [P, I], BF16, ["q_grouped1", "group_sum1", "", "inv_total0"][j])
+                picked = sb("picked%d" % j, [P, I], BF16, ["q_grouped1", "group_sum1", None, None][j])
             nc.vector.tensor_copy(picked[:], windows[j][:].indirect(offsets[:]))
-            grouped = sb("v_grouped%d" % j, [P, P * PACK], BF16)
+            grouped = sb("v_grouped%d" % j, [P, P * PACK], BF16, [None, "root0", "z2", "root1"][j])
             turn_words(picked, bank("v_turned%d" % j, "v%d" % (j % 2), [P, 2, P]), grouped)
             return grouped
 
@@ -205,7 +205,7 @@ def tile_attend_beyondgroup_typical_atleast_pl_kernel(
                 scale=mean_scale[:, h : h + 1],
                 accum_out=centre[:],
             )
-            z2 = sb("z2_%d" % h, [P, I], F32)
+            z2 = sb("z2_%d" % h, [P, I], F32, "z2")
             nc.scalar.activation(z2[:], scaled[:], ACT.Square, bias=centre[:], scale=-float(I))
             root = sb("root%d" % h, [P, I], F32)
             nc.scalar.activation(root[:], z2[:], ACT.Abs_reciprocal_sqrt, bias=one[:])
@@ -220,7 +220,10 @@ def tile_attend_beyondgroup_typical_atleast_pl_kernel(
         def weights(h, part, total):
             inv_total = sb("inv_total%d" % h, [P, 1], F32)
             nc.vector.reciprocal(inv_total[:], total[:])
-            w = sb("w%d" % h, [P, I], BF16)
+            if h == 1:
+                w = slots.tile([P, I], BF16, name="w1", tag="c")
+            else:
+                w = sb("w0", [P, I], BF16)
             nc.vector.scalar_tensor_tensor(
                 w[:],
                 part[:],
@@ -240,7 +243,7 @@ def tile_attend_beyondgroup_typical_atleast_pl_kernel(
         y = sb("y", [P, PACK, Q], F32)
         y_rows = out_0.rearrange("(p j) q -> p j q", j=PACK)
 
-        def finish(name, tag, js, cols, floor):
+        def finish(name, tag, js, cols, floor, after):
             n = cols.stop - cols.start
             shape = [P, len(js), n]
             acc = bank("o_" + name, tag, shape)
@@ -255,7 +258,7 @@ def tile_attend_beyondgroup_typical_atleast_pl_kernel(
                     stop=True,
                 )
             larger = sb("larger_" + name, shape, F32)
-            smaller = sb("smaller_" + name, shape, F32)
+            smaller = sb("smaller_" + name, shape, F32, after)
             rows = slice(js[0], js[-1] + 1)
             nc.vector.tensor_tensor(smaller[:], acc[:], floor, ALU.min)
             nc.vector.tensor_tensor(larger[:], acc[:], floor, ALU.max)
@@ -287,14 +290,13 @@ def tile_attend_beyondgroup_typical_atleast_pl_kernel(
         w0 = weights(0, *part0)
         quantize_vals(2, g2)
         quantize_weights(0, w0)
-        finish("a", "s0", [0, 1, 2], slice(0, P), floor[:, 0:3, 0:P])
         g3 = gather_vals(3)
         w1 = weights(1, *part1)
         quantize_vals(3, g3)
-        finish("b", "t0", [3], slice(0, P), floor[:, 3:4, 0:P])
         quantize_weights(1, w1)
+        finish("a", "s0", [0, 1, 2, 3], slice(0, P), floor[:, :, 0:P], "part1")
         planes(0, nc.scalar.copy)
-        finish("c", "s1", [0, 1, 2, 3], slice(P, Q), floor[:, :, P:Q])
+        finish("b", "s1", [0, 1, 2, 3], slice(P, Q), floor[:, :, P:Q], None)
         planes(1, nc.vector.tensor_copy)
         for quad in range(4):
             queue = nc.sync if quad % 2 else nc.scalar

@@ -161,10 +161,10 @@ def tile_attend_beyondgroup_typical_atleast_pl_kernel(
         inv_width = sb("inv_width", [P, HALVES], F32, "q_grouped0")
         nc.vector.reciprocal(inv_width[:], lam_col[:, HALVES : 2 * HALVES])
         mean_scale = sb("mean_scale", [P, HALVES], F32)
-        nc.vector.tensor_scalar(mean_scale[:], inv_width[:], -1.0 / I, None, ALU.mult)
+        nc.scalar.activation(mean_scale[:], inv_width[:], ACT.Copy, scale=-1.0 / I)
         rest_turned = bank("rest_turned", "v1", [P, P])
         nc.tensor.transpose(rest_turned[:], rest_rows[:], ident[:])
-        rest_col = sb("rest_col", [P, PACK], F32, "group_sum0")
+        rest_col = sb("rest_col", [P, PACK], F32, "share1")
         nc.scalar.copy(rest_col[:], rest_turned[:, 0:PACK])
         os_row = bank("os_row", "os", [P, PACK, P])
         for t in range(PACK):
@@ -182,12 +182,12 @@ def tile_attend_beyondgroup_typical_atleast_pl_kernel(
             )
 
         def gather_vals(j):
-            if j == 2:
-                picked = slots.tile([P, I], BF16, name="picked2", tag="e")
+            if j in (1, 2):
+                picked = slots.tile([P, I], BF16, name="picked%d" % j, tag="de"[j - 1])
             else:
-                picked = sb("picked%d" % j, [P, I], BF16, ["q_grouped1", "group_sum1", None, None][j])
+                picked = sb("picked%d" % j, [P, I], BF16, ["group_sum1", None, None, None][j])
             nc.vector.tensor_copy(picked[:], windows[j][:].indirect(offsets[:]))
-            grouped = sb("v_grouped%d" % j, [P, P * PACK], BF16, [None, "root0", "z2", "root1"][j])
+            grouped = sb("v_grouped%d" % j, [P, P * PACK], BF16, ["scaled0", "root0", "z2", "root1"][j])
             turn_words(picked, bank("v_turned%d" % j, "v%d" % (j % 2), [P, 2, P]), grouped)
             return grouped
 
@@ -240,7 +240,6 @@ def tile_attend_beyondgroup_typical_atleast_pl_kernel(
             cols = slice(h * P, (h + 1) * P)
             nc.vector.quantize_mx(out=w_codes[:, cols].bitcast(FP8X4), scales=w_scales[:, cols], in_=grouped[:])
 
-        y = sb("y", [P, PACK, Q], F32)
         y_rows = out_0.rearrange("(p j) q -> p j q", j=PACK)
 
         def finish(name, tag, js, cols, floor, after):
@@ -280,9 +279,9 @@ def tile_attend_beyondgroup_typical_atleast_pl_kernel(
             )
             nc.sync.dma_start(code_rows[:, cols], y_codes[:, cols].bitcast(I32))
 
-        g0 = gather_vals(0)
         part0 = parts(0)
         part1 = parts(1)
+        g0 = gather_vals(0)
         g1 = gather_vals(1)
         quantize_vals(0, g0)
         g2 = gather_vals(2)
@@ -294,6 +293,7 @@ def tile_attend_beyondgroup_typical_atleast_pl_kernel(
         w1 = weights(1, *part1)
         quantize_vals(3, g3)
         quantize_weights(1, w1)
+        y = sb("y", [P, PACK, Q], F32)
         finish("a", "s0", [0, 1, 2, 3], slice(0, P), floor[:, :, 0:P], "part1")
         planes(0, nc.scalar.copy)
         finish("b", "s1", [0, 1, 2, 3], slice(P, Q), floor[:, :, P:Q], None)

from contextlib import ExitStack

import concourse.mybir as mybir
from concourse.masks import make_identity

D, T, I, Q, E, GROUP = 512, 2048, 512, 256, 512, 8
FLOPS = 2 * D * I * Q + 2 * I * E * Q

F32 = mybir.dt.float32
BF16 = mybir.dt.bfloat16
I32 = mybir.dt.int32
U32 = mybir.dt.uint32
U16 = mybir.dt.uint16
U8 = mybir.dt.uint8
FP8X4 = mybir.dt.float8_e4m3fn_x4
FP4X4 = mybir.dt.float4_e2m1fn_x4
ALU = mybir.AluOpType
ACT = mybir.ActivationFunctionType
AX = mybir.AxisListType

P = 128
PACK = 4
HALVES = Q // P


def tile_attend_beyondgroup_typical_atleast_pl_kernel(
    tc, query, keys_words, keys_scales, lam, width, slot_factor, vals, floors, offs, out_0, out_1, out_2
):
    nc = tc.nc
    with ExitStack() as ctx:
        held = ctx.enter_context(tc.tile_pool(name="held", bufs=1))
        slots = ctx.enter_context(tc.tile_pool(name="slots", bufs=1))
        psum = ctx.enter_context(tc.psum_pool(name="psum", bufs=1))

        def sb(name, shape, dtype, tag=None):
            return held.tile(shape, dtype, name=name, tag=tag or name, align_bytes=64)

        def bank(name, tag, shape):
            return psum.tile(shape, F32, name=name, tag=tag)

        offsets = held.tile([P, I // 16], U16, name="offsets")
        nc.sync.dma_start(offsets[:], offs)

        lam_rows = sb("lam_rows", [P, P], F32)
        nc.gpsimd.memset(lam_rows[:], 0.0)
        nc.scalar.dma_start(lam_rows[0:2, :], lam.rearrange("o (h m) -> (o h) m", m=P))
        nc.gpsimd.dma_start(lam_rows[2:4, :], width.rearrange("(h m) o -> h (m o)", m=P))
        key_scales = slots.tile([P, T], U8, name="key_scales", tag="b")
        nc.vector.memset(key_scales[:].bitcast(I32), 0)
        key_words = slots.tile([P, T], U16, name="key_words", tag="a")
        nc.sync.dma_start(key_words[:].bitcast(I32), keys_words[0].bitcast(I32))
        for quad in range(4):
            nc.sync.dma_start(
                key_scales[32 * quad : 32 * quad + 4, :].bitcast(I32),
                keys_scales[0, 4 * quad : 4 * quad + 4, :].bitcast(I32),
            )
        q_raw = slots.tile([P, PACK, Q], F32, name="q_raw", tag="c")
        nc.sync.dma_start(q_raw[:], query.rearrange("(p t) q -> p t q", t=PACK))

        vals_rows = vals.rearrange("(p j) t -> j p t", j=PACK)
        windows = []

        def load_vals(j, tag):
            window = slots.tile([P, T], F32, name="vals%d" % j, tag=tag)
            nc.sync.dma_start(window[:], vals_rows[j])
            windows.append(window)

        one = sb("one", [P, 1], F32)
        nc.vector.memset(one[:], 1.0)
        seed = slots.tile([P, 1], F32, name="seed", tag="e")
        nc.vector.memset(seed[:], 1.0)
        warm = slots.tile([P, 1], F32, name="warm", tag="d")
        nc.scalar.activation(warm[:], seed[:], ACT.Abs_reciprocal_sqrt, bias=one[:])
        load_vals(0, "d")
        load_vals(1, "e")

        rest_rows = sb("rest_rows", [P, P], F32)
        ident = sb("ident", [P, P], F32)
        make_identity(nc, ident[:])
        nc.gpsimd.memset(rest_rows[:], 0.0)
        nc.gpsimd.dma_start(rest_rows[0:4, :], slot_factor.rearrange("o (c m) -> (o c) m", m=P))
        lam_turned = bank("lam_turned", "t0", [P, P])
        nc.tensor.transpose(lam_turned[:], lam_rows[:], ident[:])
        lam_col = sb("lam_col", [P, 2 * HALVES], F32)
        nc.scalar.copy(lam_col[:], lam_turned[:, 0 : 2 * HALVES])
        lam_row = bank("lam_row", "lam", [P, HALVES, P])
        for h in range(HALVES):
            nc.tensor.transpose(lam_row[:, h, :], lam_col[:, h : h + 1].to_broadcast([P, P]), ident[:])

        k_words = sb("k_words", [P, I], U16)
        k_scales = sb("k_scales", [P, I], U8)
        nc.vector.tensor_copy(k_words[:], key_words[:].indirect(offsets[:]))
        nc.vector.tensor_copy(k_scales[:], key_scales[:].indirect(offsets[:]))
        load_vals(2, "a")

        q_codes = sb("q_codes", [P, Q], U32)
        q_scales = sb("q_scales", [P, Q], U8)
        q_grouped = []
        for h in range(HALVES):
            g = sb("q_grouped%d" % h, [P, P, PACK], BF16)
            nc.scalar.copy(g[:], q_raw[:, :, h * P : (h + 1) * P].rearrange("p t q -> p q t"))
            q_grouped.append(g)
        for h in range(HALVES):
            cols = slice(h * P, (h + 1) * P)
            nc.vector.quantize_mx(
                out=q_codes[:, cols].bitcast(FP8X4),
                scales=q_scales[:, cols],
                in_=q_grouped[h][:].rearrange("p q t -> p (q t)"),
            )

        load_vals(3, "c")
        floor_rows = floors.rearrange("(p j) q -> p j q", j=PACK)
        floor = slots.tile([P, PACK, Q], F32, name="floor", tag="b")
        nc.sync.dma_start(floor[:], floor_rows)

        scores = []
        for h in range(HALVES):
            cols = slice(h * P, (h + 1) * P)
            acc = bank("scores%d" % h, "s%d" % h, [P, PACK, P])
            for c in range(PACK):
                nc.tensor.matmul_mx(
                    out=acc[:, c, :],
                    lhsT=k_words[:, c * P : (c + 1) * P].bitcast(FP4X4),
                    lhsT_scale=k_scales[:, c * P : (c + 1) * P],
                    rhs=q_codes[:, cols].bitcast(FP8X4),
                    rhs_scale=q_scales[:, cols],
                    start=True,
                    stop=True,
                )
            scores.append(acc)

        turned = []
        for h in range(HALVES):
            group_sum = sb("group_sum%d" % h, [P, PACK, P // GROUP], F32)
            nc.vector.tensor_reduce(
                group_sum[:], scores[h][:].rearrange("p c (v j) -> p c v j", j=GROUP), AX.X, ALU.add
            )
            minus_a0 = sb("minus_a0%d" % h, [P, PACK, P], F32)
            nc.scalar.activation(minus_a0[:], scores[h][:], ACT.Copy, scale=-1.0)
            share = sb("share%d" % h, [P, PACK, P], F32)
            nc.vector.tensor_tensor(
                share[:].rearrange("p c (v j) -> p c v j", j=GROUP),
                group_sum[:].unsqueeze(3).to_broadcast([P, PACK, P // GROUP, GROUP]),
                lam_row[:, h, :]
                .rearrange("p (v j) -> p v j", j=GROUP)
                .unsqueeze(1)
                .to_broadcast([P, PACK, P // GROUP, GROUP]),
                ALU.mult,
            )
            acc = bank("turned%d" % h, "t%d" % h, [P, PACK, P])
            for c in range(PACK):
                nc.tensor.matmul(
                    acc[:, c, :], minus_a0[:, c, :], ident[:], start=(c == 0), stop=False, is_transpose=True
                )
            for c in range(PACK):
                nc.tensor.matmul(
                    acc[:, c, :], share[:, c, :], ident[:], start=False, stop=(c == PACK - 1), is_transpose=True
                )
            turned.append(acc)

        inv_width = sb("inv_width", [P, HALVES], F32, "q_grouped0")
        nc.vector.reciprocal(inv_width[:], lam_col[:, HALVES : 2 * HALVES])
        mean_scale = sb("mean_scale", [P, HALVES], F32)
        nc.scalar.activation(mean_scale[:], inv_width[:], ACT.Copy, scale=-1.0 / I)
        rest_turned = bank("rest_turned", "v1", [P, P])
        nc.tensor.transpose(rest_turned[:], rest_rows[:], ident[:])
        rest_col = sb("rest_col", [P, PACK], F32, "share1")
        nc.scalar.copy(rest_col[:], rest_turned[:, 0:PACK])
        os_row = bank("os_row", "os", [P, PACK, P])
        for t in range(PACK):
            nc.tensor.transpose(os_row[:, t, :], rest_col[:, t : t + 1].to_broadcast([P, P]), ident[:])

        v_codes = sb("v_codes", [P, E], U32)
        v_scales = sb("v_scales", [P, E], U8)

        def turn_words(src, acc, dst):
            words = src[:].bitcast(F32)
            for u in range(2):
                nc.tensor.transpose(acc[:, u, :], words[:, u : I // 2 : 2], ident[:])
            nc.scalar.copy(
                dst[:].bitcast(F32).rearrange("p (m u) -> p m u", u=2), acc[:].rearrange("p u m -> p m u")
            )

        def gather_vals(j):
            if j in (1, 2):
                picked = slots.tile([P, I], BF16, name="picked%d" % j, tag="de"[j - 1])
            else:
                picked = sb("picked%d" % j, [P, I], BF16, ["group_sum1", None, None, None][j])
            nc.vector.tensor_copy(picked[:], windows[j][:].indirect(offsets[:]))
            grouped = sb("v_grouped%d" % j, [P, P * PACK], BF16, ["scaled0", "root0", "z2", "root1"][j])
            turn_words(picked, bank("v_turned%d" % j, "v%d" % (j % 2), [P, 2, P]), grouped)
            return grouped

        def quantize_vals(j, grouped):
            cols = slice(j * P, (j + 1) * P)
            nc.vector.quantize_mx(out=v_codes[:, cols].bitcast(FP8X4), scales=v_scales[:, cols], in_=grouped[:])

        def parts(h):
            scaled = sb("scaled%d" % h, [P, I], F32)
            centre = sb("centre%d" % h, [P, 1], F32)
            nc.scalar.activation(
                scaled[:],
                turned[h][:].rearrange("p c m -> p (c m)"),
                ACT.Identity,
                scale=mean_scale[:, h : h + 1],
                accum_out=centre[:],
            )
            z2 = sb("z2_%d" % h, [P, I], F32, "z2")
            nc.scalar.activation(z2[:], scaled[:], ACT.Square, bias=centre[:], scale=-float(I))
            root = sb("root%d" % h, [P, I], F32)
            nc.scalar.activation(root[:], z2[:], ACT.Abs_reciprocal_sqrt, bias=one[:])
            part = sb("part%d" % h, [P, I], F32)
            total = sb("total%d" % h, [P, 1], F32)
            nc.scalar.activation(part[:], root[:], ACT.Square, accum_out=total[:])
            return part, total

        w_codes = sb("w_codes", [P, Q], U32)
        w_scales = sb("w_scales", [P, Q], U8)

        def weights(h, part, total):
            inv_total = sb("inv_total%d" % h, [P, 1], F32)
            nc.vector.reciprocal(inv_total[:], total[:])
            if h == 1:
                w = slots.tile([P, I], BF16, name="w1", tag="c")
            else:
                w = sb("w0", [P, I], BF16)
            nc.vector.scalar_tensor_tensor(
                w[:],
                part[:],
                inv_total[:],
                os_row[:].rearrange("p c m -> p (c m)"),
                ALU.mult,
                ALU.mult,
            )
            grouped = sb("w_grouped%d" % h, [P, P * PACK], BF16)
            turn_words(w, bank("w_turned%d" % h, "lam", [P, 2, P]), grouped)
            return grouped

        def quantize_weights(h, grouped):
            cols = slice(h * P, (h + 1) * P)
            nc.vector.quantize_mx(out=w_codes[:, cols].bitcast(FP8X4), scales=w_scales[:, cols], in_=grouped[:])

        y_rows = out_0.rearrange("(p j) q -> p j q", j=PACK)

        def finish(name, tag, js, cols, floor, after):
            n = cols.stop - cols.start
            shape = [P, len(js), n]
            acc = bank("o_" + name, tag, shape)
            for k, j in enumerate(js):
                nc.tensor.matmul_mx(
                    out=acc[:, k, :],
                    lhsT=v_codes[:, j * P : (j + 1) * P].bitcast(FP8X4),
                    lhsT_scale=v_scales[:, j * P : (j + 1) * P],
                    rhs=w_codes[:, cols].bitcast(FP8X4),
                    rhs_scale=w_scales[:, cols],
                    start=True,
                    stop=True,
                )
            larger = sb("larger_" + name, shape, F32)
            smaller = sb("smaller_" + name, shape, F32, after)
            rows = slice(js[0], js[-1] + 1)
            nc.vector.tensor_tensor(smaller[:], acc[:], floor, ALU.min)
            nc.vector.tensor_tensor(larger[:], acc[:], floor, ALU.max)
            nc.vector.scalar_tensor_tensor(y[:, rows, cols], smaller[:], 0.1, larger[:], ALU.mult, ALU.add)
            nc.sync.dma_start(y_rows[:, rows, cols], y[:, rows, cols])

        y_codes = sb("y_codes", [P, Q], U32)
        y_scales = sb("y_scales", [P, Q], U8)
        code_rows = out_1[0].rearrange("p c t -> p (c t)").bitcast(I32)

        def planes(h, copy):
            cols = slice(h * P, (h + 1) * P)
            grouped = sb("y_grouped%d" % h, [P, P, PACK], BF16)
            copy(grouped[:], y[:, :, cols].rearrange("p j q -> p q j"))
            nc.vector.quantize_mx(
                out=y_codes[:, cols].bitcast(FP8X4),
                scales=y_scales[:, cols],
                in_=grouped[:].rearrange("p q j -> p (q j)"),
            )
            nc.sync.dma_start(code_rows[:, cols], y_codes[:, cols].bitcast(I32))

        part0 = parts(0)
        part1 = parts(1)
        g0 = gather_vals(0)
        g1 = gather_vals(1)
        quantize_vals(0, g0)
        g2 = gather_vals(2)
        quantize_vals(1, g1)
        w0 = weights(0, *part0)
        quantize_vals(2, g2)
        quantize_weights(0, w0)
        g3 = gather_vals(3)
        w1 = weights(1, *part1)
        quantize_vals(3, g3)
        quantize_weights(1, w1)
        y = sb("y", [P, PACK, Q], F32)
        finish("a", "s0", [0, 1, 2, 3], slice(0, P), floor[:, :, 0:P], "part1")
        planes(0, nc.scalar.copy)
        finish("b", "s1", [0, 1, 2, 3], slice(P, Q), floor[:, :, P:Q], None)
        planes(1, nc.vector.tensor_copy)
        for quad in range(4):
            queue = nc.sync if quad % 2 else nc.scalar
            queue.dma_start(
                out_2[0, 4 * quad : 4 * quad + 4, :].bitcast(I32),
                y_scales[32 * quad : 32 * quad + 4, :].bitcast(I32),
            )
